import numpy as np
import ml_dtypes


def mxq(x, axis, fmt="e4m3"):
    dtype, down = {"e4m3": (ml_dtypes.float8_e4m3fn, 7), "e5m2": (ml_dtypes.float8_e5m2, 14)}[fmt]
    v = np.moveaxis(np.asarray(x, np.float32).astype(ml_dtypes.bfloat16).astype(np.float64), axis, -1)
    blocks = v.reshape(v.shape[:-1] + (-1, 32))
    amax = np.abs(blocks).max(-1, keepdims=True)
    byte = np.maximum(np.where(amax > 0, np.frexp(amax)[1] - 1 + 127, 0) - down, 1)
    scale = np.exp2(byte - 127.0)
    codes = (blocks / scale).astype(np.float32).astype(dtype).astype(np.float64)
    return np.moveaxis((codes * scale).reshape(v.shape), -1, axis)


WIDE = False


def mx_kscale(k):
    if not WIDE:
        return np.ones(k)
    levels = np.array([10, -10, 5, -5, 0])
    if k % 512:
        return np.exp2(np.random.permutation(np.resize(levels, k // 32))).repeat(32)
    a = np.empty((k // 512, 16))
    for p in range(k // 512):
        a[p, :8] = np.random.permutation(np.resize(levels, 8))
        for g in range(8):
            far = levels[np.abs(levels - a[p, g]) >= 10]
            a[p, g + 8] = far[np.random.randint(len(far))]
    return np.exp2(a.ravel()).repeat(32)


def f64(x):
    return np.asarray(x).astype(np.float64)


def striped(idx):
    return np.tile(idx.reshape(-1, 16).T, (8, 1)).astype(np.uint16)


def unstriped(offs):
    return offs[:16].T.reshape(-1).astype(np.int64)


def pack_weight(w):
    k, n = w.shape
    w = f64(np.asarray(w, np.float32).astype(ml_dtypes.bfloat16)).reshape(k // 32, 32, n)
    amax = np.abs(w).max(1)
    byte = np.clip(np.where(amax > 0, np.frexp(amax)[1] - 1 + 127 - 7, 1), 1, 254)
    scaled = (w * np.exp2(127.0 - byte)[:, None, :]).reshape(k, n).astype(np.float32)
    words = np.ascontiguousarray(scaled.reshape(k // 512, 128, 4, n).transpose(0, 1, 3, 2)).astype(ml_dtypes.float8_e4m3fn).view(np.uint8)
    return words, np.ascontiguousarray(byte.astype(np.uint8).reshape(k // 512, 16, n))


def unpack_weight(words, scales):
    g, p, n, _ = words.shape
    vals = np.ascontiguousarray(words).view(ml_dtypes.float8_e4m3fn).astype(np.float64) * np.repeat(np.exp2(scales.astype(np.float64) - 127.0), 8, axis=1)[..., None]
    return vals.transpose(0, 1, 3, 2).reshape(g * 512, n)


def silu(v):
    return v / (1.0 + np.exp(-np.maximum(v, -700.0)))


K, T, S, N, H = 1024, 2048, 512, 128, 512


def setup_inputs():
    n = np.random.standard_normal
    s = mx_kscale(K)[:, None]
    c = mx_kscale(S)
    packed_xT = pack_weight(n((K, T)) * s)
    return {
        "x_words": packed_xT[0],
        "x_scales": packed_xT[1],
        "py": (n((K, H)) / np.sqrt(K) / s).astype(np.float32),
        "pzz1": (n((K, N)) / np.sqrt(K) / s).astype(np.float32),
        "wa": (np.random.uniform(0.4, 1.0, (S, 1)) * c[:, None] / np.sqrt(S)).astype(np.float32),
        "wb": (np.random.uniform(0.6, 1.4, (S, 1)) / c[:, None]).astype(np.float32),
        "mom": (n((H, N))).astype(np.float32),
        "offs": striped(np.random.permutation(T)[:S]),
    }


def reference(x_words, x_scales, py, pzz1, wa, wb, mom, offs):
    xq = unpack_weight(x_words, x_scales)[:, unstriped(offs)]
    pyq = mxq(f64(py), 0, "e4m3")
    y = xq.T @ pyq
    ya = np.tanh(y)
    ka = f64(wa) * ya
    pzz1q = mxq(f64(pzz1), 0, "e4m3")
    zz1 = xq.T @ pzz1q
    zb = silu(zz1)
    kv = f64(wb) * zb
    gr = mxq(ka, 0, "e4m3").T @ mxq(kv, 0, "e4m3")
    mnew = 0.7 * f64(mom) + gr
    m2 = (mnew) ** 2
    rowm = m2.mean(axis=1, keepdims=True)
    return mnew / np.sqrt(rowm + 0.1)

@@ -1,0 +1,194 @@
+import math
+from contextlib import ExitStack
+
+import concourse.mybir as mybir
+
+K, T, S, N, H = 1024, 2048, 512, 128, 512
+FLOPS = 2 * K * S * (H + N) + 2 * S * H * N
+
+F32 = mybir.dt.float32
+BF16 = mybir.dt.bfloat16
+I32 = mybir.dt.int32
+U32 = mybir.dt.uint32
+U16 = mybir.dt.uint16
+U8 = mybir.dt.uint8
+FP8X4 = mybir.dt.float8_e4m3fn_x4
+ACT = mybir.ActivationFunctionType
+ALU = mybir.AluOpType
+
+P = 128
+PACK = 4
+K_PASS = P * PACK
+PASSES = K // K_PASS
+W = 128
+CHUNKS = H // W
+
+
+def tile_picked_yshamp_silu_p_kernel(
+    tc, x_words, x_scales, py, pzz1, wa, wb, mom, offs, out
+):
+    nc = tc.nc
+    with ExitStack() as ctx:
+        keep = ctx.enter_context(tc.tile_pool(name="keep", bufs=1))
+        psum = ctx.enter_context(tc.psum_pool(name="psum", bufs=1))
+
+        def sb(name, shape, dtype):
+            return keep.tile(shape, dtype, name=name, align_bytes=64)
+
+        offsets = keep.tile([P, S // 16], U16, name="offsets")
+        nc.sync.dma_start(offsets[:], offs)
+
+        xs_all = sb("xs_all", [P, T], U8)
+        nc.gpsimd.memset(xs_all[:].bitcast(I32), 0)
+        for q in range(4):
+            nc.gpsimd.dma_start(
+                xs_all[32 * q : 32 * q + 4 * PASSES, :].bitcast(I32),
+                x_scales[:, 4 * q : 4 * q + 4, :].bitcast(I32),
+            )
+
+        pz_raw = sb("pz_raw", [P, PASSES, PACK, N], F32)
+        nc.sync.dma_start(
+            pz_raw[:].rearrange("p o j n -> p o (j n)"),
+            pzz1.rearrange("(o p j) n -> p o (j n)", o=PASSES, j=PACK),
+        )
+        xw_all = []
+        for o in range(PASSES):
+            t = sb("xw_all%d" % o, [P, T], U32)
+            nc.sync.dma_start(t[:].bitcast(I32), x_words[o].rearrange("p n t -> p (n t)").bitcast(I32))
+            xw_all.append(t)
+
+        py_rows = py.rearrange("(o p j) n -> o p j n", o=PASSES, j=PACK)
+        py_raw = {}
+
+        def load_py(o, c0, c1):
+            t = sb("py_raw%d_%d" % (o, c0), [P, PACK, (c1 - c0) * W], F32)
+            nc.sync.dma_start(t[:], py_rows[o, :, :, c0 * W : c1 * W])
+            for c in range(c0, c1):
+                py_raw[o, c] = t[:, :, (c - c0) * W : (c - c0 + 1) * W]
+
+        load_py(0, 0, 2)
+        load_py(1, 0, 2)
+        load_py(0, 2, 4)
+        load_py(1, 2, 3)
+        load_py(1, 3, 4)
+
+        wa_t = sb("wa_t", [P, PACK], F32)
+        wb_t = sb("wb_t", [P, PACK], F32)
+        nc.scalar.dma_start(wa_t[:], wa.rearrange("(p j) one -> p (j one)", j=PACK))
+        nc.scalar.dma_start(wb_t[:], wb.rearrange("(p j) one -> p (j one)", j=PACK))
+
+        mom_t = sb("mom_t", [P, CHUNKS, N], F32)
+        nc.sync.dma_start(mom_t[:], mom.rearrange("(c p) m -> p c m", p=P))
+
+        ones = sb("ones", [P, 1], F32)
+        nc.vector.memset(ones[:], 1.0)
+        half = sb("half", [P, 1], F32)
+        nc.gpsimd.memset(half[:], -0.5)
+        mnew = []
+        for c in range(CHUNKS):
+            t = sb("mnew%d" % c, [P, N + 1], F32)
+            nc.vector.tensor_scalar(t[:, N : N + 1], ones[:], math.sqrt(0.1 * N), None, ALU.mult)
+            mnew.append(t)
+
+        def interleave(name, raw, on_scalar):
+            g = sb(name, [P, W, PACK], BF16)
+            view = raw.rearrange("p j n -> p n j")
+            if on_scalar:
+                nc.scalar.copy(g[:], view)
+            else:
+                nc.vector.tensor_copy(g[:], view)
+            return g
+
+        def quantize(name, g):
+            codes = sb(name + "_c", [P, W], U32)
+            scales = sb(name + "_s", [P, W], U8)
+            nc.vector.quantize_mx(codes[:].bitcast(FP8X4), scales[:], g[:].rearrange("p n j -> p (n j)"))
+            return codes, scales
+
+        def project(bank, o, operand):
+            codes, scales = operand
+            for j in range(PACK):
+                nc.tensor.matmul_mx(
+                    bank[:, j, :],
+                    lhsT=xw[o][:, j, :].bitcast(FP8X4),
+                    lhsT_scale=xs[4 * o :, j, :],
+                    rhs=codes[:].bitcast(FP8X4),
+                    rhs_scale=scales[:],
+                    start=(o == 0 and j == 0),
+                    stop=(o == PASSES - 1 and j == PACK - 1),
+                )
+
+        def activate(name, bank, func):
+            t = sb(name, [P, W, PACK], F32)
+            nc.scalar.activation(t[:], bank[:].rearrange("p j n -> p n j"), func)
+            return t
+
+        def weigh(name, t, w):
+            g = sb(name, [P, W, PACK], BF16)
+            nc.vector.tensor_tensor(g[:], t[:], w[:].unsqueeze(1).to_broadcast([P, W, PACK]), ALU.mult)
+            return g
+
+        pz_g = [interleave("pz_g%d" % o, pz_raw[:, o], True) for o in range(PASSES)]
+        pz_q = [quantize("pz_q%d" % o, pz_g[o]) for o in range(PASSES)]
+
+        xw = [sb("xw%d" % o, [P, PACK, P], U32) for o in range(PASSES)]
+        xs = sb("xs", [P, PACK, P], U8)
+        nc.vector.tensor_copy(xw[0][:].rearrange("p j m -> p m j"), xw_all[0][:].indirect(offsets[:]))
+        nc.vector.tensor_copy(xs[:].rearrange("p j m -> p m j"), xs_all[:].indirect(offsets[:]))
+        nc.vector.tensor_copy(xw[1][:].rearrange("p j m -> p m j"), xw_all[1][:].indirect(offsets[:]))
+
+        z_bank = psum.tile([P, PACK, W], F32, name="z_bank")
+        for o in range(PASSES):
+            project(z_bank, o, pz_q[o])
+        zb = activate("zb", z_bank, ACT.Silu)
+
+        y_bank = [psum.tile([P, PACK, W], F32, name="y_bank%d" % c) for c in range(CHUNKS)]
+        g_bank = [psum.tile([P, N], F32, name="g_bank%d" % b) for b in range(3)]
+        on_scalar = {(0, 1), (1, 1), (0, 2), (0, 3)}
+
+        def first_product(c, o):
+            g = interleave("py_g%d_%d" % (o, c), py_raw[o, c], (o, c) in on_scalar)
+            project(y_bank[c], o, quantize("py_q%d_%d" % (o, c), g))
+
+        def second_product(c):
+            ya = activate("ya%d" % c, y_bank[c], ACT.Tanh)
+            ka_c, ka_s = quantize("ka_q%d" % c, weigh("ka%d" % c, ya, wa_t))
+            nc.tensor.matmul_mx(
+                g_bank[c % 3][:],
+                lhsT=ka_c[:].bitcast(FP8X4),
+                lhsT_scale=ka_s[:],
+                rhs=kv_c[:].bitcast(FP8X4),
+                rhs_scale=kv_s[:],
+                start=True,
+                stop=True,
+            )
+
+        def finish(c):
+            m = mnew[c]
+            nc.vector.scalar_tensor_tensor(m[:, :N], mom_t[:, c, :], 0.7, g_bank[c % 3][:], ALU.mult, ALU.add)
+            sq = sb("sq%d" % c, [P, N + 1], F32)
+            ms = sb("ms%d" % c, [P, 1], F32)
+            nc.scalar.activation(sq[:], m[:], ACT.Square, scale=1.0 / math.sqrt(N), accum_out=ms[:])
+            rs = sb("rs%d" % c, [P, 1], F32)
+            nc.gpsimd.tensor_tensor(rs[:], ms[:], half[:], ALU.pow)
+            res = sb("res%d" % c, [P, N], F32)
+            nc.scalar.activation(res[:], m[:, :N], ACT.Copy, scale=rs[:])
+            nc.sync.dma_start(out[c * P : (c + 1) * P, :], res[:])
+
+        first_product(0, 0)
+        first_product(1, 0)
+        kv_c, kv_s = quantize("kv_q", weigh("kv", zb, wb_t))
+        first_product(0, 1)
+        first_product(1, 1)
+        second_product(0)
+        first_product(2, 0)
+        first_product(3, 0)
+        second_product(1)
+        first_product(2, 1)
+        finish(0)
+        first_product(3, 1)
+        second_product(2)
+        finish(1)
+        second_product(3)
+        finish(2)
+        finish(3)

@@ -1,4 +1,3 @@
-import math
 from contextlib import ExitStack
 
 import concourse.mybir as mybir
@@ -32,29 +31,30 @@ def tile_picked_yshamp_silu_p_kernel(
         keep = ctx.enter_context(tc.tile_pool(name="keep", bufs=1))
         psum = ctx.enter_context(tc.psum_pool(name="psum", bufs=1))
 
-        def sb(name, shape, dtype):
-            return keep.tile(shape, dtype, name=name, align_bytes=64)
+        def sb(name, shape, dtype, tag=None):
+            return keep.tile(shape, dtype, name=name, tag=tag or name, align_bytes=64)
 
         offsets = keep.tile([P, S // 16], U16, name="offsets")
         nc.sync.dma_start(offsets[:], offs)
 
         xs_all = sb("xs_all", [P, T], U8)
-        nc.gpsimd.memset(xs_all[:].bitcast(I32), 0)
-        for q in range(4):
-            nc.gpsimd.dma_start(
-                xs_all[32 * q : 32 * q + 4 * PASSES, :].bitcast(I32),
-                x_scales[:, 4 * q : 4 * q + 4, :].bitcast(I32),
-            )
+        nc.vector.memset(xs_all[:].bitcast(I32), 0)
 
         pz_raw = sb("pz_raw", [P, PASSES, PACK, N], F32)
         nc.sync.dma_start(
             pz_raw[:].rearrange("p o j n -> p o (j n)"),
             pzz1.rearrange("(o p j) n -> p o (j n)", o=PASSES, j=PACK),
         )
+        for q in range(4):
+            nc.sync.dma_start(
+                xs_all[32 * q : 32 * q + 4 * PASSES, :].bitcast(I32),
+                x_scales[:, 4 * q : 4 * q + 4, :].bitcast(I32),
+            )
         xw_all = []
         for o in range(PASSES):
             t = sb("xw_all%d" % o, [P, T], U32)
-            nc.sync.dma_start(t[:].bitcast(I32), x_words[o].rearrange("p n t -> p (n t)").bitcast(I32))
+            words = x_words[o].rearrange("p n t -> p (n t)").bitcast(I32)
+            nc.sync.dma_start(t[:].bitcast(I32), words)
             xw_all.append(t)
 
         py_rows = py.rearrange("(o p j) n -> o p j n", o=PASSES, j=PACK)
@@ -64,7 +64,7 @@ def tile_picked_yshamp_silu_p_kernel(
             t = sb("py_raw%d_%d" % (o, c0), [P, PACK, (c1 - c0) * W], F32)
             nc.sync.dma_start(t[:], py_rows[o, :, :, c0 * W : c1 * W])
             for c in range(c0, c1):
-                py_raw[o, c] = t[:, :, (c - c0) * W : (c - c0 + 1) * W]
+                py_raw[o, c] = (t, (c - c0) * W)
 
         load_py(0, 0, 2)
         load_py(1, 0, 2)
@@ -74,21 +74,11 @@ def tile_picked_yshamp_silu_p_kernel(
 
         wa_t = sb("wa_t", [P, PACK], F32)
         wb_t = sb("wb_t", [P, PACK], F32)
-        nc.scalar.dma_start(wa_t[:], wa.rearrange("(p j) one -> p (j one)", j=PACK))
-        nc.scalar.dma_start(wb_t[:], wb.rearrange("(p j) one -> p (j one)", j=PACK))
+        nc.gpsimd.dma_start(wa_t[:], wa.rearrange("(p j) one -> p (j one)", j=PACK))
+        nc.gpsimd.dma_start(wb_t[:], wb.rearrange("(p j) one -> p (j one)", j=PACK))
 
         mom_t = sb("mom_t", [P, CHUNKS, N], F32)
         nc.sync.dma_start(mom_t[:], mom.rearrange("(c p) m -> p c m", p=P))
-
-        ones = sb("ones", [P, 1], F32)
-        nc.vector.memset(ones[:], 1.0)
-        half = sb("half", [P, 1], F32)
-        nc.gpsimd.memset(half[:], -0.5)
-        mnew = []
-        for c in range(CHUNKS):
-            t = sb("mnew%d" % c, [P, N + 1], F32)
-            nc.vector.tensor_scalar(t[:, N : N + 1], ones[:], math.sqrt(0.1 * N), None, ALU.mult)
-            mnew.append(t)
 
         def interleave(name, raw, on_scalar):
             g = sb(name, [P, W, PACK], BF16)
@@ -99,62 +89,81 @@ def tile_picked_yshamp_silu_p_kernel(
                 nc.vector.tensor_copy(g[:], view)
             return g
 
-        def quantize(name, g):
-            codes = sb(name + "_c", [P, W], U32)
-            scales = sb(name + "_s", [P, W], U8)
+        def quantize(name, g, width=W):
+            codes = sb(name + "_c", [P, width], U32)
+            scales = sb(name + "_s", [P, width], U8)
             nc.vector.quantize_mx(codes[:].bitcast(FP8X4), scales[:], g[:].rearrange("p n j -> p (n j)"))
             return codes, scales
 
-        def project(bank, o, operand):
-            codes, scales = operand
+        def project(bank, o, codes, scales):
             for j in range(PACK):
                 nc.tensor.matmul_mx(
                     bank[:, j, :],
                     lhsT=xw[o][:, j, :].bitcast(FP8X4),
                     lhsT_scale=xs[4 * o :, j, :],
-                    rhs=codes[:].bitcast(FP8X4),
-                    rhs_scale=scales[:],
+                    rhs=codes.bitcast(FP8X4),
+                    rhs_scale=scales,
                     start=(o == 0 and j == 0),
                     stop=(o == PASSES - 1 and j == PACK - 1),
                 )
 
-        def activate(name, bank, func):
-            t = sb(name, [P, W, PACK], F32)
+        def activate(name, bank, func, tag=None):
+            t = sb(name, [P, W, PACK], F32, tag)
             nc.scalar.activation(t[:], bank[:].rearrange("p j n -> p n j"), func)
             return t
 
-        def weigh(name, t, w):
-            g = sb(name, [P, W, PACK], BF16)
+        def weigh(name, t, w, tag=None):
+            g = sb(name, [P, W, PACK], BF16, tag)
             nc.vector.tensor_tensor(g[:], t[:], w[:].unsqueeze(1).to_broadcast([P, W, PACK]), ALU.mult)
             return g
 
-        pz_g = [interleave("pz_g%d" % o, pz_raw[:, o], True) for o in range(PASSES)]
+        pz_g = [interleave("pz_g%d" % o, pz_raw[:, o], False) for o in range(PASSES)]
         pz_q = [quantize("pz_q%d" % o, pz_g[o]) for o in range(PASSES)]
 
         xw = [sb("xw%d" % o, [P, PACK, P], U32) for o in range(PASSES)]
         xs = sb("xs", [P, PACK, P], U8)
-        nc.vector.tensor_copy(xw[0][:].rearrange("p j m -> p m j"), xw_all[0][:].indirect(offsets[:]))
         nc.vector.tensor_copy(xs[:].rearrange("p j m -> p m j"), xs_all[:].indirect(offsets[:]))
+        nc.vector.tensor_copy(xw[0][:].rearrange("p j m -> p m j"), xw_all[0][:].indirect(offsets[:]))
         nc.vector.tensor_copy(xw[1][:].rearrange("p j m -> p m j"), xw_all[1][:].indirect(offsets[:]))
 
-        z_bank = psum.tile([P, PACK, W], F32, name="z_bank")
+        z_bank = psum.tile([P, PACK, W], F32, name="z_bank", tag="z_bank")
         for o in range(PASSES):
-            project(z_bank, o, pz_q[o])
+            project(z_bank, o, pz_q[o][0][:], pz_q[o][1][:])
         zb = activate("zb", z_bank, ACT.Silu)
 
         y_bank = [psum.tile([P, PACK, W], F32, name="y_bank%d" % c) for c in range(CHUNKS)]
-        g_bank = [psum.tile([P, N], F32, name="g_bank%d" % b) for b in range(3)]
-        on_scalar = {(0, 1), (1, 1), (0, 2), (0, 3)}
+        g_bank = {}
+        def staging(o, c0, c1):
+            return sb("py_g%d_%d" % (o, c0), [P, (c1 - c0) * W, PACK], BF16)
 
-        def first_product(c, o):
-            g = interleave("py_g%d_%d" % (o, c), py_raw[o, c], (o, c) in on_scalar)
-            project(y_bank[c], o, quantize("py_q%d_%d" % (o, c), g))
+        def lay_out(g, o, c, lo, hi, on_scalar):
+            raw, base = py_raw[o, c]
+            view = raw[:, :, base + lo : base + hi].rearrange("p j n -> p n j")
+            if on_scalar:
+                nc.scalar.copy(g[:, lo:hi, :], view)
+            else:
+                nc.vector.tensor_copy(g[:, lo:hi, :], view)
+
+        def first_product(g, o, c0, c1):
+            codes, scales = quantize("py_q%d_%d" % (o, c0), g, (c1 - c0) * W)
+            for c in range(c0, c1):
+                cols = slice((c - c0) * W, (c - c0 + 1) * W)
+                project(y_bank[c], o, codes[:, cols], scales[:, cols])
+
+        ya = {}
+        ka = {}
+
+        def squash(c):
+            ya[c] = activate("ya%d" % c, y_bank[c], ACT.Tanh, "py_raw1_2" if c == 0 else None)
+
+        def weigh_ka(c):
+            ka[c] = weigh("ka%d" % c, ya[c], wa_t, "py_g1_3" if c == 0 else None)
 
         def second_product(c):
-            ya = activate("ya%d" % c, y_bank[c], ACT.Tanh)
-            ka_c, ka_s = quantize("ka_q%d" % c, weigh("ka%d" % c, ya, wa_t))
+            ka_c, ka_s = quantize("ka_q%d" % c, ka[c])
+            g_bank[c] = psum.tile([P, N], F32, name="g_bank%d" % c, tag="z_bank" if c == 3 else "g_bank%d" % c)
             nc.tensor.matmul_mx(
-                g_bank[c % 3][:],
+                g_bank[c][:],
                 lhsT=ka_c[:].bitcast(FP8X4),
                 lhsT_scale=ka_s[:],
                 rhs=kv_c[:].bitcast(FP8X4),
@@ -163,32 +172,62 @@ def tile_picked_yshamp_silu_p_kernel(
                 stop=True,
             )
 
-        def finish(c):
-            m = mnew[c]
-            nc.vector.scalar_tensor_tensor(m[:, :N], mom_t[:, c, :], 0.7, g_bank[c % 3][:], ALU.mult, ALU.add)
-            sq = sb("sq%d" % c, [P, N + 1], F32)
-            ms = sb("ms%d" % c, [P, 1], F32)
-            nc.scalar.activation(sq[:], m[:], ACT.Square, scale=1.0 / math.sqrt(N), accum_out=ms[:])
-            rs = sb("rs%d" % c, [P, 1], F32)
-            nc.gpsimd.tensor_tensor(rs[:], ms[:], half[:], ALU.pow)
-            res = sb("res%d" % c, [P, N], F32)
-            nc.scalar.activation(res[:], m[:, :N], ACT.Copy, scale=rs[:])
-            nc.sync.dma_start(out[c * P : (c + 1) * P, :], res[:])
+        mnew = [sb("mnew%d" % c, [P, N], F32) for c in range(CHUNKS)]
+        ss = sb("ss", [P, CHUNKS], F32)
 
-        first_product(0, 0)
-        first_product(1, 0)
-        kv_c, kv_s = quantize("kv_q", weigh("kv", zb, wb_t))
-        first_product(0, 1)
-        first_product(1, 1)
+        def moment(c):
+            nc.vector.scalar_tensor_tensor(mnew[c][:], mom_t[:, c, :], 0.7, g_bank[c][:], ALU.mult, ALU.add)
+            sq = sb("sq%d" % c, [P, N], F32)
+            nc.scalar.activation(sq[:], mnew[c][:], ACT.Square, accum_out=ss[:, c : c + 1])
+
+        def normalise(c0, c1, on_scalar):
+            nc.scalar.activation(rs[:, c0:c1], ss[:, c0:c1], ACT.Abs_reciprocal_sqrt, bias=0.1, scale=1.0 / N)
+            for c in range(c0, c1):
+                res = sb("res%d" % c, [P, N], F32)
+                if on_scalar:
+                    nc.scalar.activation(res[:], mnew[c][:], ACT.Copy, scale=rs[:, c : c + 1])
+                else:
+                    nc.vector.tensor_scalar(res[:], mnew[c][:], rs[:, c : c + 1], None, ALU.mult)
+                nc.sync.dma_start(out[c * P : (c + 1) * P, :], res[:])
+
+        g_a0 = staging(0, 0, 2)
+        lay_out(g_a0, 0, 0, 0, 2 * W, False)
+        first_product(g_a0, 0, 0, 2)
+        g_10 = staging(1, 0, 1)
+        g_11 = staging(1, 1, 2)
+        lay_out(g_10, 1, 0, 0, W, False)
+        lay_out(g_11, 1, 1, 0, W, False)
+        first_product(g_10, 1, 0, 1)
+        first_product(g_11, 1, 1, 2)
+        g_b0 = staging(0, 2, 4)
+        lay_out(g_b0, 0, 2, 0, W, True)
+        lay_out(g_b0, 0, 2, W, 2 * W, False)
+        g_12 = staging(1, 2, 3)
+        lay_out(g_12, 1, 2, 0, W, True)
+        kv = weigh("kv", zb, wb_t, "py_g1_1")
+        first_product(g_b0, 0, 2, 4)
+        g_13 = staging(1, 3, 4)
+        lay_out(g_13, 1, 3, 0, W, False)
+        first_product(g_12, 1, 2, 3)
+        first_product(g_13, 1, 3, 4)
+        squash(0)
+        squash(1)
+        squash(2)
+        squash(3)
+        kv_c, kv_s = quantize("kv_q", kv)
+        weigh_ka(0)
+        weigh_ka(1)
         second_product(0)
-        first_product(2, 0)
-        first_product(3, 0)
+        weigh_ka(2)
         second_product(1)
-        first_product(2, 1)
-        finish(0)
-        first_product(3, 1)
+        weigh_ka(3)
         second_product(2)
-        finish(1)
         second_product(3)
-        finish(2)
-        finish(3)
+        moment(0)
+        rs = sb("rs", [P, CHUNKS], F32, tag="py_q1_3_c")
+        normalise(0, 1, False)
+        moment(1)
+        moment(2)
+        moment(3)
+        normalise(1, 3, False)
+        normalise(3, 4, True)

@@ -57,6 +57,11 @@ def tile_picked_yshamp_silu_p_kernel(
             nc.sync.dma_start(t[:].bitcast(I32), words)
             xw_all.append(t)
 
+        wa_t = sb("wa_t", [P, PACK], F32)
+        wb_t = sb("wb_t", [P, PACK], F32)
+        nc.sync.dma_start(wa_t[:], wa.rearrange("(p j) one -> p (j one)", j=PACK))
+        nc.sync.dma_start(wb_t[:], wb.rearrange("(p j) one -> p (j one)", j=PACK))
+
         py_rows = py.rearrange("(o p j) n -> o p j n", o=PASSES, j=PACK)
         py_raw = {}
 
@@ -71,11 +76,6 @@ def tile_picked_yshamp_silu_p_kernel(
         load_py(0, 2, 4)
         load_py(1, 2, 3)
         load_py(1, 3, 4)
-
-        wa_t = sb("wa_t", [P, PACK], F32)
-        wb_t = sb("wb_t", [P, PACK], F32)
-        nc.gpsimd.dma_start(wa_t[:], wa.rearrange("(p j) one -> p (j one)", j=PACK))
-        nc.gpsimd.dma_start(wb_t[:], wb.rearrange("(p j) one -> p (j one)", j=PACK))
 
         mom_t = sb("mom_t", [P, CHUNKS, N], F32)
         nc.sync.dma_start(mom_t[:], mom.rearrange("(c p) m -> p c m", p=P))

@@ -35,7 +35,6 @@ def tile_picked_yshamp_silu_p_kernel(
             return keep.tile(shape, dtype, name=name, tag=tag or name, align_bytes=64)
 
         offsets = keep.tile([P, S // 16], U16, name="offsets")
-        nc.sync.dma_start(offsets[:], offs)
 
         xs_all = sb("xs_all", [P, T], U8)
         nc.vector.memset(xs_all[:].bitcast(I32), 0)
@@ -50,6 +49,7 @@ def tile_picked_yshamp_silu_p_kernel(
                 xs_all[32 * q : 32 * q + 4 * PASSES, :].bitcast(I32),
                 x_scales[:, 4 * q : 4 * q + 4, :].bitcast(I32),
             )
+        nc.sync.dma_start(offsets[:], offs)
         xw_all = []
         for o in range(PASSES):
             t = sb("xw_all%d" % o, [P, T], U32)
@@ -74,20 +74,18 @@ def tile_picked_yshamp_silu_p_kernel(
         load_py(0, 0, 2)
         load_py(1, 0, 2)
         load_py(0, 2, 4)
-        load_py(1, 2, 3)
-        load_py(1, 3, 4)
+        load_py(1, 2, 4)
 
         mom_t = sb("mom_t", [P, CHUNKS, N], F32)
         nc.sync.dma_start(mom_t[:], mom.rearrange("(c p) m -> p c m", p=P))
 
-        def interleave(name, raw, on_scalar):
-            g = sb(name, [P, W, PACK], BF16)
-            view = raw.rearrange("p j n -> p n j")
+        def interleave(dst, src, on_scalar):
+            dst = dst.rearrange("p (c i) j -> p c j i", i=4)
+            src = src.rearrange("p j (c i) -> p c j i", i=4)
             if on_scalar:
-                nc.scalar.copy(g[:], view)
+                nc.scalar.copy(dst, src)
             else:
-                nc.vector.tensor_copy(g[:], view)
-            return g
+                nc.vector.tensor_copy(dst, src)
 
         def quantize(name, g, width=W):
             codes = sb(name + "_c", [P, width], U32)
@@ -117,8 +115,10 @@ def tile_picked_yshamp_silu_p_kernel(
             nc.vector.tensor_tensor(g[:], t[:], w[:].unsqueeze(1).to_broadcast([P, W, PACK]), ALU.mult)
             return g
 
-        pz_g = [interleave("pz_g%d" % o, pz_raw[:, o], False) for o in range(PASSES)]
-        pz_q = [quantize("pz_q%d" % o, pz_g[o]) for o in range(PASSES)]
+        pz_g = sb("pz_g", [P, PASSES * N, PACK], BF16)
+        for o in range(PASSES):
+            interleave(pz_g[:, o * N : (o + 1) * N, :], pz_raw[:, o], False)
+        pz_c, pz_s = quantize("pz_q", pz_g, PASSES * N)
 
         xw = [sb("xw%d" % o, [P, PACK, P], U32) for o in range(PASSES)]
         xs = sb("xs", [P, PACK, P], U8)
@@ -128,7 +128,7 @@ def tile_picked_yshamp_silu_p_kernel(
 
         z_bank = psum.tile([P, PACK, W], F32, name="z_bank", tag="z_bank")
         for o in range(PASSES):
-            project(z_bank, o, pz_q[o][0][:], pz_q[o][1][:])
+            project(z_bank, o, pz_c[:, o * N : (o + 1) * N], pz_s[:, o * N : (o + 1) * N])
         zb = activate("zb", z_bank, ACT.Silu)
 
         y_bank = [psum.tile([P, PACK, W], F32, name="y_bank%d" % c) for c in range(CHUNKS)]
@@ -138,11 +138,7 @@ def tile_picked_yshamp_silu_p_kernel(
 
         def lay_out(g, o, c, lo, hi, on_scalar):
             raw, base = py_raw[o, c]
-            view = raw[:, :, base + lo : base + hi].rearrange("p j n -> p n j")
-            if on_scalar:
-                nc.scalar.copy(g[:, lo:hi, :], view)
-            else:
-                nc.vector.tensor_copy(g[:, lo:hi, :], view)
+            interleave(g[:, lo:hi, :], raw[:, :, base + lo : base + hi], on_scalar)
 
         def first_product(g, o, c0, c1):
             codes, scales = quantize("py_q%d_%d" % (o, c0), g, (c1 - c0) * W)
@@ -154,10 +150,10 @@ def tile_picked_yshamp_silu_p_kernel(
         ka = {}
 
         def squash(c):
-            ya[c] = activate("ya%d" % c, y_bank[c], ACT.Tanh, "py_raw1_2" if c == 0 else None)
+            ya[c] = activate("ya%d" % c, y_bank[c], ACT.Tanh)
 
         def weigh_ka(c):
-            ka[c] = weigh("ka%d" % c, ya[c], wa_t, "py_g1_3" if c == 0 else None)
+            ka[c] = weigh("ka%d" % c, ya[c], wa_t, "py_g1_%d" % (c + 2) if c < 2 else None)
 
         def second_product(c):
             ka_c, ka_s = quantize("ka_q%d" % c, ka[c])
@@ -173,49 +169,60 @@ def tile_picked_yshamp_silu_p_kernel(
             )
 
         mnew = [sb("mnew%d" % c, [P, N], F32) for c in range(CHUNKS)]
-        ss = sb("ss", [P, CHUNKS], F32)
 
         def moment(c):
             nc.vector.scalar_tensor_tensor(mnew[c][:], mom_t[:, c, :], 0.7, g_bank[c][:], ALU.mult, ALU.add)
-            sq = sb("sq%d" % c, [P, N], F32)
-            nc.scalar.activation(sq[:], mnew[c][:], ACT.Square, accum_out=ss[:, c : c + 1])
 
-        def normalise(c0, c1, on_scalar):
-            nc.scalar.activation(rs[:, c0:c1], ss[:, c0:c1], ACT.Abs_reciprocal_sqrt, bias=0.1, scale=1.0 / N)
-            for c in range(c0, c1):
-                res = sb("res%d" % c, [P, N], F32)
-                if on_scalar:
-                    nc.scalar.activation(res[:], mnew[c][:], ACT.Copy, scale=rs[:, c : c + 1])
-                else:
-                    nc.vector.tensor_scalar(res[:], mnew[c][:], rs[:, c : c + 1], None, ALU.mult)
+        def squares(c, total, on_scalar):
+            sq = sb("sq%d" % c, [P, N], F32)
+            if on_scalar:
+                nc.scalar.activation(sq[:], mnew[c][:], ACT.Square, accum_out=total)
+            else:
+                nc.vector.scalar_tensor_tensor(
+                    sq[:], mnew[c][:], 1.0, mnew[c][:], ALU.mult, ALU.mult, accum_out=total
+                )
+
+        def inverse_root(c0, c1, totals):
+            nc.scalar.activation(rs[:, c0:c1], totals, ACT.Abs_reciprocal_sqrt, bias=0.1, scale=1.0 / N)
+
+        def normalise(c, on_scalar):
+            res = sb("res%d" % c, [P, N], F32)
+            if on_scalar:
+                nc.scalar.activation(res[:], mnew[c][:], ACT.Copy, scale=rs[:, c : c + 1])
+                nc.scalar.dma_start(out[c * P : (c + 1) * P, :], res[:])
+            else:
+                nc.vector.tensor_scalar(res[:], mnew[c][:], rs[:, c : c + 1], None, ALU.mult)
                 nc.sync.dma_start(out[c * P : (c + 1) * P, :], res[:])
 
-        g_a0 = staging(0, 0, 2)
-        lay_out(g_a0, 0, 0, 0, 2 * W, False)
-        first_product(g_a0, 0, 0, 2)
+        g_00 = staging(0, 0, 1)
+        g_01 = staging(0, 1, 2)
+        lay_out(g_00, 0, 0, 0, W, False)
+        lay_out(g_01, 0, 1, 0, W, False)
+        first_product(g_00, 0, 0, 1)
+        first_product(g_01, 0, 1, 2)
         g_10 = staging(1, 0, 1)
         g_11 = staging(1, 1, 2)
-        lay_out(g_10, 1, 0, 0, W, False)
-        lay_out(g_11, 1, 1, 0, W, False)
+        lay_out(g_10, 1, 0, 0, W, True)
+        lay_out(g_11, 1, 1, 0, W, True)
+        kv = weigh("kv", zb, wb_t, "py_g0_1")
         first_product(g_10, 1, 0, 1)
-        first_product(g_11, 1, 1, 2)
+        kv_c, kv_s = quantize("kv_q", kv)
         g_b0 = staging(0, 2, 4)
         lay_out(g_b0, 0, 2, 0, W, True)
         lay_out(g_b0, 0, 2, W, 2 * W, False)
-        g_12 = staging(1, 2, 3)
-        lay_out(g_12, 1, 2, 0, W, True)
-        kv = weigh("kv", zb, wb_t, "py_g1_1")
+        first_product(g_11, 1, 1, 2)
         first_product(g_b0, 0, 2, 4)
-        g_13 = staging(1, 3, 4)
-        lay_out(g_13, 1, 3, 0, W, False)
-        first_product(g_12, 1, 2, 3)
-        first_product(g_13, 1, 3, 4)
         squash(0)
+        g_12 = staging(1, 2, 3)
+        g_13 = staging(1, 3, 4)
+        lay_out(g_12, 1, 2, 0, W, False)
+        lay_out(g_13, 1, 3, 0, W, True)
+        first_product(g_12, 1, 2, 3)
+        weigh_ka(0)
+        first_product(g_13, 1, 3, 4)
         squash(1)
         squash(2)
         squash(3)
-        kv_c, kv_s = quantize("kv_q", kv)
-        weigh_ka(0)
         weigh_ka(1)
         second_product(0)
         weigh_ka(2)
@@ -224,10 +231,16 @@ def tile_picked_yshamp_silu_p_kernel(
         second_product(2)
         second_product(3)
         moment(0)
-        rs = sb("rs", [P, CHUNKS], F32, tag="py_q1_3_c")
-        normalise(0, 1, False)
         moment(1)
+        ss_first = sb("ss_first", [P, 1], F32, tag="ss")
+        squares(0, ss_first[:], False)
+        rs = sb("rs", [P, CHUNKS], F32, tag="ya3")
+        inverse_root(0, 1, ss_first[:])
+        ss_rest = sb("ss_rest", [P, CHUNKS - 1], F32, tag="ss")
         moment(2)
         moment(3)
-        normalise(1, 3, False)
-        normalise(3, 4, True)
+        for c in range(1, CHUNKS):
+            squares(c, ss_rest[:, c - 1 : c], True)
+        inverse_root(1, CHUNKS, ss_rest[:])
+        for c in range(CHUNKS):
+            normalise(c, c == CHUNKS - 1)

from contextlib import ExitStack

import concourse.mybir as mybir

K, T, S, N, H = 1024, 2048, 512, 128, 512
FLOPS = 2 * K * S * (H + N) + 2 * S * H * N

F32 = mybir.dt.float32
BF16 = mybir.dt.bfloat16
I32 = mybir.dt.int32
U32 = mybir.dt.uint32
U16 = mybir.dt.uint16
U8 = mybir.dt.uint8
FP8X4 = mybir.dt.float8_e4m3fn_x4
ACT = mybir.ActivationFunctionType
ALU = mybir.AluOpType

P = 128
PACK = 4
K_PASS = P * PACK
PASSES = K // K_PASS
W = 128
CHUNKS = H // W


def tile_picked_yshamp_silu_p_kernel(
    tc, x_words, x_scales, py, pzz1, wa, wb, mom, offs, out
):
    nc = tc.nc
    with ExitStack() as ctx:
        keep = ctx.enter_context(tc.tile_pool(name="keep", bufs=1))
        psum = ctx.enter_context(tc.psum_pool(name="psum", bufs=1))

        def sb(name, shape, dtype, tag=None):
            return keep.tile(shape, dtype, name=name, tag=tag or name, align_bytes=64)

        offsets = keep.tile([P, S // 16], U16, name="offsets")

        xs_all = sb("xs_all", [P, T], U8)
        nc.vector.memset(xs_all[:].bitcast(I32), 0)

        pz_raw = sb("pz_raw", [P, PASSES, PACK, N], F32)
        nc.sync.dma_start(
            pz_raw[:].rearrange("p o j n -> p o (j n)"),
            pzz1.rearrange("(o p j) n -> p o (j n)", o=PASSES, j=PACK),
        )
        for q in range(4):
            nc.sync.dma_start(
                xs_all[32 * q : 32 * q + 4 * PASSES, :].bitcast(I32),
                x_scales[:, 4 * q : 4 * q + 4, :].bitcast(I32),
            )
        nc.sync.dma_start(offsets[:], offs)
        xw_all = []
        for o in range(PASSES):
            t = sb("xw_all%d" % o, [P, T], U32)
            words = x_words[o].rearrange("p n t -> p (n t)").bitcast(I32)
            nc.sync.dma_start(t[:].bitcast(I32), words)
            xw_all.append(t)

        wa_t = sb("wa_t", [P, PACK], F32)
        wb_t = sb("wb_t", [P, PACK], F32)
        nc.sync.dma_start(wa_t[:], wa.rearrange("(p j) one -> p (j one)", j=PACK))
        nc.sync.dma_start(wb_t[:], wb.rearrange("(p j) one -> p (j one)", j=PACK))

        py_rows = py.rearrange("(o p j) n -> o p j n", o=PASSES, j=PACK)
        py_raw = {}

        def load_py(o, c0, c1):
            t = sb("py_raw%d_%d" % (o, c0), [P, PACK, (c1 - c0) * W], F32)
            nc.sync.dma_start(t[:], py_rows[o, :, :, c0 * W : c1 * W])
            for c in range(c0, c1):
                py_raw[o, c] = (t, (c - c0) * W)

        load_py(0, 0, 2)
        load_py(1, 0, 2)
        load_py(0, 2, 4)
        load_py(1, 2, 4)

        mom_t = sb("mom_t", [P, CHUNKS, N], F32)
        nc.sync.dma_start(mom_t[:], mom.rearrange("(c p) m -> p c m", p=P))

        def interleave(dst, src, on_scalar):
            dst = dst.rearrange("p (c i) j -> p c j i", i=4)
            src = src.rearrange("p j (c i) -> p c j i", i=4)
            if on_scalar:
                nc.scalar.copy(dst, src)
            else:
                nc.vector.tensor_copy(dst, src)

        def quantize(name, g, width=W):
            codes = sb(name + "_c", [P, width], U32)
            scales = sb(name + "_s", [P, width], U8)
            nc.vector.quantize_mx(codes[:].bitcast(FP8X4), scales[:], g[:].rearrange("p n j -> p (n j)"))
            return codes, scales

        def project(bank, o, codes, scales):
            for j in range(PACK):
                nc.tensor.matmul_mx(
                    bank[:, j, :],
                    lhsT=xw[o][:, j, :].bitcast(FP8X4),
                    lhsT_scale=xs[4 * o :, j, :],
                    rhs=codes.bitcast(FP8X4),
                    rhs_scale=scales,
                    start=(o == 0 and j == 0),
                    stop=(o == PASSES - 1 and j == PACK - 1),
                )

        def activate(name, bank, func, tag=None):
            t = sb(name, [P, W, PACK], F32, tag)
            nc.scalar.activation(t[:], bank[:].rearrange("p j n -> p n j"), func)
            return t

        def weigh(name, t, w, tag=None):
            g = sb(name, [P, W, PACK], BF16, tag)
            nc.vector.tensor_tensor(g[:], t[:], w[:].unsqueeze(1).to_broadcast([P, W, PACK]), ALU.mult)
            return g

        pz_g = sb("pz_g", [P, PASSES * N, PACK], BF16)
        for o in range(PASSES):
            interleave(pz_g[:, o * N : (o + 1) * N, :], pz_raw[:, o], False)
        pz_c, pz_s = quantize("pz_q", pz_g, PASSES * N)

        xw = [sb("xw%d" % o, [P, PACK, P], U32) for o in range(PASSES)]
        xs = sb("xs", [P, PACK, P], U8)
        nc.vector.tensor_copy(xs[:].rearrange("p j m -> p m j"), xs_all[:].indirect(offsets[:]))
        nc.vector.tensor_copy(xw[0][:].rearrange("p j m -> p m j"), xw_all[0][:].indirect(offsets[:]))
        nc.vector.tensor_copy(xw[1][:].rearrange("p j m -> p m j"), xw_all[1][:].indirect(offsets[:]))

        z_bank = psum.tile([P, PACK, W], F32, name="z_bank", tag="z_bank")
        for o in range(PASSES):
            project(z_bank, o, pz_c[:, o * N : (o + 1) * N], pz_s[:, o * N : (o + 1) * N])
        zb = activate("zb", z_bank, ACT.Silu)

        y_bank = [psum.tile([P, PACK, W], F32, name="y_bank%d" % c) for c in range(CHUNKS)]
        g_bank = {}
        def staging(o, c0, c1):
            return sb("py_g%d_%d" % (o, c0), [P, (c1 - c0) * W, PACK], BF16)

        def lay_out(g, o, c, lo, hi, on_scalar):
            raw, base = py_raw[o, c]
            interleave(g[:, lo:hi, :], raw[:, :, base + lo : base + hi], on_scalar)

        def first_product(g, o, c0, c1):
            codes, scales = quantize("py_q%d_%d" % (o, c0), g, (c1 - c0) * W)
            for c in range(c0, c1):
                cols = slice((c - c0) * W, (c - c0 + 1) * W)
                project(y_bank[c], o, codes[:, cols], scales[:, cols])

        ya = {}
        ka = {}

        def squash(c):
            ya[c] = activate("ya%d" % c, y_bank[c], ACT.Tanh)

        def weigh_ka(c):
            ka[c] = weigh("ka%d" % c, ya[c], wa_t, "py_g1_%d" % (c + 2) if c < 2 else None)

        def second_product(c):
            ka_c, ka_s = quantize("ka_q%d" % c, ka[c])
            g_bank[c] = psum.tile([P, N], F32, name="g_bank%d" % c, tag="z_bank" if c == 3 else "g_bank%d" % c)
            nc.tensor.matmul_mx(
                g_bank[c][:],
                lhsT=ka_c[:].bitcast(FP8X4),
                lhsT_scale=ka_s[:],
                rhs=kv_c[:].bitcast(FP8X4),
                rhs_scale=kv_s[:],
                start=True,
                stop=True,
            )

        mnew = [sb("mnew%d" % c, [P, N], F32) for c in range(CHUNKS)]

        def moment(c):
            nc.vector.scalar_tensor_tensor(mnew[c][:], mom_t[:, c, :], 0.7, g_bank[c][:], ALU.mult, ALU.add)

        def squares(c, total, on_scalar):
            sq = sb("sq%d" % c, [P, N], F32)
            if on_scalar:
                nc.scalar.activation(sq[:], mnew[c][:], ACT.Square, accum_out=total)
            else:
                nc.vector.scalar_tensor_tensor(
                    sq[:], mnew[c][:], 1.0, mnew[c][:], ALU.mult, ALU.mult, accum_out=total
                )

        def inverse_root(c0, c1, totals):
            nc.scalar.activation(rs[:, c0:c1], totals, ACT.Abs_reciprocal_sqrt, bias=0.1, scale=1.0 / N)

        def normalise(c, on_scalar):
            res = sb("res%d" % c, [P, N], F32)
            if on_scalar:
                nc.scalar.activation(res[:], mnew[c][:], ACT.Copy, scale=rs[:, c : c + 1])
                nc.scalar.dma_start(out[c * P : (c + 1) * P, :], res[:])
            else:
                nc.vector.tensor_scalar(res[:], mnew[c][:], rs[:, c : c + 1], None, ALU.mult)
                nc.sync.dma_start(out[c * P : (c + 1) * P, :], res[:])

        g_00 = staging(0, 0, 1)
        g_01 = staging(0, 1, 2)
        lay_out(g_00, 0, 0, 0, W, False)
        lay_out(g_01, 0, 1, 0, W, False)
        first_product(g_00, 0, 0, 1)
        first_product(g_01, 0, 1, 2)
        g_10 = staging(1, 0, 1)
        g_11 = staging(1, 1, 2)
        lay_out(g_10, 1, 0, 0, W, True)
        lay_out(g_11, 1, 1, 0, W, True)
        kv = weigh("kv", zb, wb_t, "py_g0_1")
        first_product(g_10, 1, 0, 1)
        kv_c, kv_s = quantize("kv_q", kv)
        g_b0 = staging(0, 2, 4)
        lay_out(g_b0, 0, 2, 0, W, True)
        lay_out(g_b0, 0, 2, W, 2 * W, False)
        first_product(g_11, 1, 1, 2)
        first_product(g_b0, 0, 2, 4)
        squash(0)
        g_12 = staging(1, 2, 3)
        g_13 = staging(1, 3, 4)
        lay_out(g_12, 1, 2, 0, W, False)
        lay_out(g_13, 1, 3, 0, W, True)
        first_product(g_12, 1, 2, 3)
        weigh_ka(0)
        first_product(g_13, 1, 3, 4)
        squash(1)
        squash(2)
        squash(3)
        weigh_ka(1)
        second_product(0)
        weigh_ka(2)
        second_product(1)
        weigh_ka(3)
        second_product(2)
        second_product(3)
        moment(0)
        moment(1)
        ss_first = sb("ss_first", [P, 1], F32, tag="ss")
        squares(0, ss_first[:], False)
        rs = sb("rs", [P, CHUNKS], F32, tag="ya3")
        inverse_root(0, 1, ss_first[:])
        ss_rest = sb("ss_rest", [P, CHUNKS - 1], F32, tag="ss")
        moment(2)
        moment(3)
        for c in range(1, CHUNKS):
            squares(c, ss_rest[:, c - 1 : c], True)
        inverse_root(1, CHUNKS, ss_rest[:])
        for c in range(CHUNKS):
            normalise(c, c == CHUNKS - 1)
